import numpy as np
import ml_dtypes


def mxq(x, axis, fmt="e4m3"):
    dtype, down = {"e4m3": (ml_dtypes.float8_e4m3fn, 7), "e5m2": (ml_dtypes.float8_e5m2, 14)}[fmt]
    v = np.moveaxis(np.asarray(x, np.float32).astype(ml_dtypes.bfloat16).astype(np.float64), axis, -1)
    blocks = v.reshape(v.shape[:-1] + (-1, 32))
    amax = np.abs(blocks).max(-1, keepdims=True)
    byte = np.maximum(np.where(amax > 0, np.frexp(amax)[1] - 1 + 127, 0) - down, 1)
    scale = np.exp2(byte - 127.0)
    codes = (blocks / scale).astype(np.float32).astype(dtype).astype(np.float64)
    return np.moveaxis((codes * scale).reshape(v.shape), -1, axis)


WIDE = False


def mx_kscale(k):
    if not WIDE:
        return np.ones(k)
    levels = np.array([10, -10, 5, -5, 0])
    if k % 512:
        return np.exp2(np.random.permutation(np.resize(levels, k // 32))).repeat(32)
    a = np.empty((k // 512, 16))
    for p in range(k // 512):
        a[p, :8] = np.random.permutation(np.resize(levels, 8))
        for g in range(8):
            far = levels[np.abs(levels - a[p, g]) >= 10]
            a[p, g + 8] = far[np.random.randint(len(far))]
    return np.exp2(a.ravel()).repeat(32)


def f64(x):
    return np.asarray(x).astype(np.float64)


def striped(idx):
    return np.tile(idx.reshape(-1, 16).T, (8, 1)).astype(np.uint16)


def unstriped(offs):
    return offs[:16].T.reshape(-1).astype(np.int64)


def gelu(v):
    return 0.5 * v * (1.0 + np.tanh(np.sqrt(2.0 / np.pi) * (v + 0.044715 * v**3)))


K, T, H, N = 1024, 128, 512, 256


def setup_inputs():
    n = np.random.standard_normal
    s = mx_kscale(K)[:, None]
    u = mx_kscale(H)
    idx = np.random.permutation(H)
    v = np.empty(H)
    v[idx] = u
    return {
        "xT": (n((K, T)) * s).astype(np.float32),
        "w1": (n((K, H)) / np.sqrt(K) / s * v).astype(np.float32),
        "w2": (n((H, N)) / np.sqrt(H) / u[:, None]).astype(np.float32),
        "offs": striped(idx),
    }


def reference(xT, w1, w2, offs):
    idx = unstriped(offs)
    h = gelu(mxq(f64(w1), 0, "e4m3").T @ mxq(f64(xT), 0, "e4m3"))
    return mxq(f64(w2), 0, "e4m3").T @ mxq(h[idx], 0, "e4m3")

@@ -1,0 +1,158 @@
+from contextlib import ExitStack
+
+import concourse.mybir as mybir
+from concourse.masks import make_identity
+
+K, T, H, N = 1024, 128, 512, 256
+FLOPS = 2 * K * T * H + 2 * H * T * N
+
+F32 = mybir.dt.float32
+BF16 = mybir.dt.bfloat16
+U32 = mybir.dt.uint32
+U16 = mybir.dt.uint16
+U8 = mybir.dt.uint8
+FP8X4 = mybir.dt.float8_e4m3fn_x4
+GELU = mybir.ActivationFunctionType.Gelu_apprx_tanh
+COPY = mybir.ActivationFunctionType.Copy
+
+P = 128
+PACK = 4
+KP = 512
+
+PIECES = ((0, 256), (256, 128), (384, 128))
+
+
+def interleave(engine_copy, dst, raw, c0, c1):
+    engine_copy(
+        dst[:, PACK * c0 : PACK * c1].rearrange("p (c i j) -> p c j i", i=4, j=PACK),
+        raw[:, :, c0:c1].rearrange("p j (c i) -> p c j i", i=4),
+    )
+
+
+def tile_picked_shuffle_mlp_gelu_perm_l_kernel(tc, xT, w1, w2, offs, out):
+    nc = tc.nc
+
+    def vcopy(dst, src):
+        nc.vector.tensor_copy(out=dst, in_=src)
+
+    def scopy(dst, src):
+        nc.scalar.copy(dst, src)
+
+    def quantize(codes, scales, grouped):
+        nc.vector.quantize_mx(out=codes.bitcast(FP8X4), scales=scales, in_=grouped)
+
+    with ExitStack() as ctx:
+        keep = ctx.enter_context(tc.tile_pool(name="keep", bufs=1))
+        psum = ctx.enter_context(tc.psum_pool(name="psum", bufs=1))
+
+        offsets = keep.tile([P, H // 16], U16, name="offsets")
+        x_raw = keep.tile([P, 2, PACK, T], F32, name="x_raw")
+        w1_raw0 = keep.tile([P, PACK, H], F32, name="w1_raw0")
+        w1_raw1a = keep.tile([P, PACK, 384], F32, name="w1_raw1a")
+        w1_raw1b = keep.tile([P, PACK, 128], F32, name="w1_raw1b")
+        w2_raw = keep.tile([P, PACK, N], F32, name="w2_raw")
+
+        nc.sync.dma_start(out=x_raw[:], in_=xT.rearrange("(g p j) t -> p g j t", g=2, j=PACK))
+        nc.sync.dma_start(out=w1_raw0[:], in_=w1[0:KP, :].rearrange("(p j) c -> p j c", j=PACK))
+        w1_hi = w1[KP:K, :].rearrange("(p j) c -> p j c", j=PACK)
+        nc.sync.dma_start(out=w1_raw1a[:], in_=w1_hi[:, :, 0:384])
+        nc.sync.dma_start(out=w1_raw1b[:], in_=w1_hi[:, :, 384:512])
+        nc.sync.dma_start(offsets[:], offs)
+        nc.sync.dma_start(out=w2_raw[:], in_=w2.rearrange("(p j) m -> p j m", j=PACK))
+
+        warm = keep.tile([P, 1], F32, name="warm")
+        warm_out = keep.tile([P, 1], F32, name="warm_out")
+        nc.vector.memset(warm[:], 0.0)
+        nc.scalar.activation(warm_out[:], warm[:], GELU)
+
+        ident = keep.tile([P, P], F32, name="ident")
+        make_identity(nc, ident[:])
+
+        x_bf = keep.tile([P, 2 * T * PACK], BF16, name="x_bf", align_bytes=64)
+        x_codes = keep.tile([P, 2 * T], U32, name="x_codes", align_bytes=64)
+        x_scales = keep.tile([P, 2 * T], U8, name="x_scales", align_bytes=64)
+        for g, copy in ((0, vcopy), (1, scopy)):
+            interleave(copy, x_bf[:, g * T * PACK : (g + 1) * T * PACK], x_raw[:, g], 0, T)
+        quantize(x_codes[:], x_scales[:], x_bf[:])
+
+        w1_bf = keep.tile([P, 2, H * PACK], BF16, name="w1_bf", align_bytes=64)
+        w1_codes = keep.tile([P, 2, H], U32, name="w1_codes", align_bytes=64)
+        w1_scales = keep.tile([P, 2, H], U8, name="w1_scales", align_bytes=64)
+        interleave(vcopy, w1_bf[:, 0], w1_raw0, 0, 320)
+        interleave(scopy, w1_bf[:, 0], w1_raw0, 320, 512)
+        quantize(w1_codes[:, 0, :], w1_scales[:, 0, :], w1_bf[:, 0, :])
+
+        acc = []
+        for c0, width in PIECES:
+            bank = psum.tile([P, 512], F32, name="acc%d" % c0)
+            acc.append(bank)
+
+        def pass_k(g, index):
+            c0, width = PIECES[index]
+            nc.tensor.matmul_mx(
+                out=acc[index][:, 0:width],
+                lhsT=x_codes[:, g * T : (g + 1) * T].bitcast(FP8X4),
+                lhsT_scale=x_scales[:, g * T : (g + 1) * T],
+                rhs=w1_codes[:, g, c0 : c0 + width].bitcast(FP8X4),
+                rhs_scale=w1_scales[:, g, c0 : c0 + width],
+                start=(g == 0),
+                stop=(g == 1),
+            )
+
+        for index in range(len(PIECES)):
+            pass_k(0, index)
+
+        h = keep.tile([P, H], F32, name="h", align_bytes=64)
+
+        def w1_piece(index, raw, r0, split):
+            c0, width = PIECES[index]
+            base = w1_bf[:, 1, PACK * (c0 - r0) : PACK * (c0 - r0) + PACK * (r0 + width)]
+            interleave(vcopy, base, raw, r0, r0 + split)
+            interleave(scopy, base, raw, r0 + split, r0 + width)
+            quantize(w1_codes[:, 1, c0 : c0 + width], w1_scales[:, 1, c0 : c0 + width], w1_bf[:, 1, PACK * c0 : PACK * (c0 + width)])
+            pass_k(1, index)
+            nc.scalar.activation(h[:, c0 : c0 + width], acc[index][:, 0:width], GELU)
+
+        w1_piece(0, w1_raw1a, 0, 160)
+        w1_piece(1, w1_raw1a, 256, 80)
+        w1_piece(2, w1_raw1b, 0, 80)
+
+        g_bf = keep.tile([P, H], BF16, name="g_bf", align_bytes=64)
+        g_view = g_bf[:].rearrange("q (u p e) -> q p u e", u=2, e=2)
+        for half in range(2):
+            nc.vector.tensor_copy(
+                out=g_view[:, 64 * half : 64 * (half + 1)],
+                in_=h[:].indirect(offsets[:, 16 * half : 16 * (half + 1)]),
+            )
+
+        w2_bf = keep.tile([P, N * PACK], BF16, name="w2_bf", align_bytes=64)
+        w2_codes = keep.tile([P, N], U32, name="w2_codes", align_bytes=64)
+        w2_scales = keep.tile([P, N], U8, name="w2_scales", align_bytes=64)
+        interleave(scopy, w2_bf, w2_raw, 0, N)
+        quantize(w2_codes[:], w2_scales[:], w2_bf[:])
+
+        words = g_bf[:].bitcast(F32)
+        turned = psum.tile([P, 2, P], F32, name="turned")
+        for u in range(2):
+            nc.tensor.transpose(turned[:, u, :], words[:, 128 * u : 128 * (u + 1)], ident[:])
+        h_bf = keep.tile([P, T * PACK], BF16, name="h_bf", align_bytes=64)
+        nc.scalar.copy(h_bf[:].bitcast(F32).rearrange("p (t u) -> p t u", u=2), turned[:].rearrange("p u t -> p t u"))
+        h_codes = keep.tile([P, T], U32, name="h_codes", align_bytes=64)
+        h_scales = keep.tile([P, T], U8, name="h_scales", align_bytes=64)
+        quantize(h_codes[:], h_scales[:], h_bf[:])
+
+        for m, copy, dma in ((0, vcopy, nc.sync), (1, scopy, nc.scalar)):
+            bank = psum.tile([P, 512], F32, name="out_bank%d" % m)
+            cols = slice(P * m, P * (m + 1))
+            nc.tensor.matmul_mx(
+                out=bank[:, 0:T],
+                lhsT=w2_codes[:, cols].bitcast(FP8X4),
+                lhsT_scale=w2_scales[:, cols],
+                rhs=h_codes[:].bitcast(FP8X4),
+                rhs_scale=h_scales[:],
+                start=True,
+                stop=True,
+            )
+            y = keep.tile([P, T], F32, name="y%d" % m)
+            copy(y[:], bank[:, 0:T])
+            dma.dma_start(out=out[cols, :], in_=y[:])

@@ -14,20 +14,13 @@ U8 = mybir.dt.uint8
 FP8X4 = mybir.dt.float8_e4m3fn_x4
 GELU = mybir.ActivationFunctionType.Gelu_apprx_tanh
 COPY = mybir.ActivationFunctionType.Copy
+MULT, ADD = mybir.AluOpType.mult, mybir.AluOpType.add
 
 P = 128
 PACK = 4
 KP = 512
 
 PIECES = ((0, 256), (256, 128), (384, 128))
-
-
-def interleave(engine_copy, dst, raw, c0, c1):
-    engine_copy(
-        dst[:, PACK * c0 : PACK * c1].rearrange("p (c i j) -> p c j i", i=4, j=PACK),
-        raw[:, :, c0:c1].rearrange("p j (c i) -> p c j i", i=4),
-    )
-
 
 def tile_picked_shuffle_mlp_gelu_perm_l_kernel(tc, xT, w1, w2, offs, out):
     nc = tc.nc
@@ -37,6 +30,15 @@ def tile_picked_shuffle_mlp_gelu_perm_l_kernel(tc, xT, w1, w2, offs, out):
 
     def scopy(dst, src):
         nc.scalar.copy(dst, src)
+
+    def gcopy(dst, src):
+        nc.gpsimd.tensor_scalar(out=dst, in0=src, scalar1=1.0, scalar2=0.0, op0=MULT, op1=ADD)
+
+    def interleave(copy, dst, raw, c0, c1, j0=0, j1=PACK):
+        copy(
+            dst.rearrange("p (c i j) -> p c j i", i=4, j=PACK)[:, c0 // 4 : c1 // 4, j0:j1],
+            raw[:, j0:j1, c0:c1].rearrange("p j (c i) -> p c j i", i=4),
+        )
 
     def quantize(codes, scales, grouped):
         nc.vector.quantize_mx(out=codes.bitcast(FP8X4), scales=scales, in_=grouped)
@@ -48,15 +50,22 @@ def tile_picked_shuffle_mlp_gelu_perm_l_kernel(tc, xT, w1, w2, offs, out):
         offsets = keep.tile([P, H // 16], U16, name="offsets")
         x_raw = keep.tile([P, 2, PACK, T], F32, name="x_raw")
         w1_raw0 = keep.tile([P, PACK, H], F32, name="w1_raw0")
-        w1_raw1a = keep.tile([P, PACK, 384], F32, name="w1_raw1a")
-        w1_raw1b = keep.tile([P, PACK, 128], F32, name="w1_raw1b")
+        w1_raw1 = []
+        for c0, width in PIECES:
+            raw = keep.tile([P, PACK, width], F32, name="w1_raw1_%d" % c0, tag="h" if c0 == 384 else "raw%d" % c0, align_bytes=64)
+            w1_raw1.append(raw)
         w2_raw = keep.tile([P, PACK, N], F32, name="w2_raw")
 
-        nc.sync.dma_start(out=x_raw[:], in_=xT.rearrange("(g p j) t -> p g j t", g=2, j=PACK))
-        nc.sync.dma_start(out=w1_raw0[:], in_=w1[0:KP, :].rearrange("(p j) c -> p j c", j=PACK))
+        w1_lo = w1[0:KP, :].rearrange("(p j) c -> p j c", j=PACK)
+        nc.sync.dma_start(out=x_raw[:, 0], in_=xT[0:KP, :].rearrange("(p j) t -> p j t", j=PACK))
+        nc.sync.dma_start(out=w1_raw0[:, 0:2], in_=w1_lo[:, 0:2])
+        nc.sync.dma_start(out=w1_raw0[:, 2:4], in_=w1_lo[:, 2:4])
+        nc.sync.dma_start(out=x_raw[:, 1], in_=xT[KP:K, :].rearrange("(p j) t -> p j t", j=PACK))
         w1_hi = w1[KP:K, :].rearrange("(p j) c -> p j c", j=PACK)
-        nc.sync.dma_start(out=w1_raw1a[:], in_=w1_hi[:, :, 0:384])
-        nc.sync.dma_start(out=w1_raw1b[:], in_=w1_hi[:, :, 384:512])
+        nc.sync.dma_start(out=w1_raw1[0][:, 0:2], in_=w1_hi[:, 0:2, 0:256])
+        nc.sync.dma_start(out=w1_raw1[0][:, 2:4], in_=w1_hi[:, 2:4, 0:256])
+        nc.sync.dma_start(out=w1_raw1[1][:], in_=w1_hi[:, :, 256:384])
+        nc.sync.dma_start(out=w1_raw1[2][:], in_=w1_hi[:, :, 384:512])
         nc.sync.dma_start(offsets[:], offs)
         nc.sync.dma_start(out=w2_raw[:], in_=w2.rearrange("(p j) m -> p j m", j=PACK))
 
@@ -71,16 +80,23 @@ def tile_picked_shuffle_mlp_gelu_perm_l_kernel(tc, xT, w1, w2, offs, out):
         x_bf = keep.tile([P, 2 * T * PACK], BF16, name="x_bf", align_bytes=64)
         x_codes = keep.tile([P, 2 * T], U32, name="x_codes", align_bytes=64)
         x_scales = keep.tile([P, 2 * T], U8, name="x_scales", align_bytes=64)
-        for g, copy in ((0, vcopy), (1, scopy)):
-            interleave(copy, x_bf[:, g * T * PACK : (g + 1) * T * PACK], x_raw[:, g], 0, T)
-        quantize(x_codes[:], x_scales[:], x_bf[:])
-
         w1_bf = keep.tile([P, 2, H * PACK], BF16, name="w1_bf", align_bytes=64)
         w1_codes = keep.tile([P, 2, H], U32, name="w1_codes", align_bytes=64)
         w1_scales = keep.tile([P, 2, H], U8, name="w1_scales", align_bytes=64)
-        interleave(vcopy, w1_bf[:, 0], w1_raw0, 0, 320)
-        interleave(scopy, w1_bf[:, 0], w1_raw0, 320, 512)
+
+        def quantize_x(g):
+            cols = slice(g * T, (g + 1) * T)
+            quantize(x_codes[:, cols], x_scales[:, cols], x_bf[:, PACK * g * T : PACK * (g + 1) * T])
+
+        interleave(scopy, x_bf[:, 0 : T * PACK], x_raw[:, 0], 0, T)
+        quantize_x(0)
+        for j0 in (0, 2):
+            interleave(vcopy, w1_bf[:, 0], w1_raw0, 0, 320, j0, j0 + 2)
+            interleave(scopy, w1_bf[:, 0], w1_raw0, 320, H, j0, j0 + 2)
         quantize(w1_codes[:, 0, :], w1_scales[:, 0, :], w1_bf[:, 0, :])
+        interleave(vcopy, x_bf[:, T * PACK :], x_raw[:, 1], 0, 64)
+        interleave(scopy, x_bf[:, T * PACK :], x_raw[:, 1], 64, T)
+        quantize_x(1)
 
         acc = []
         for c0, width in PIECES:
@@ -99,36 +115,55 @@ def tile_picked_shuffle_mlp_gelu_perm_l_kernel(tc, xT, w1, w2, offs, out):
                 stop=(g == 1),
             )
 
+        def quantize_piece(index):
+            c0, width = PIECES[index]
+            cols = slice(c0, c0 + width)
+            quantize(w1_codes[:, 1, cols], w1_scales[:, 1, cols], w1_bf[:, 1, PACK * c0 : PACK * (c0 + width)])
+
         for index in range(len(PIECES)):
             pass_k(0, index)
 
-        h = keep.tile([P, H], F32, name="h", align_bytes=64)
+        h = keep.tile([P, H], F32, name="h", tag="h", align_bytes=64)
+        hb = keep.tile([P, H], BF16, name="hb", align_bytes=64)
 
-        def w1_piece(index, raw, r0, split):
+        def interleave_piece(index, vector_columns, j0=0, j1=PACK):
             c0, width = PIECES[index]
-            base = w1_bf[:, 1, PACK * (c0 - r0) : PACK * (c0 - r0) + PACK * (r0 + width)]
-            interleave(vcopy, base, raw, r0, r0 + split)
-            interleave(scopy, base, raw, r0 + split, r0 + width)
-            quantize(w1_codes[:, 1, c0 : c0 + width], w1_scales[:, 1, c0 : c0 + width], w1_bf[:, 1, PACK * c0 : PACK * (c0 + width)])
-            pass_k(1, index)
-            nc.scalar.activation(h[:, c0 : c0 + width], acc[index][:, 0:width], GELU)
+            dst = w1_bf[:, 1, PACK * c0 : PACK * (c0 + width)]
+            interleave(vcopy, dst, w1_raw1[index], 0, vector_columns, j0, j1)
+            interleave(scopy, dst, w1_raw1[index], vector_columns, width, j0, j1)
 
-        w1_piece(0, w1_raw1a, 0, 160)
-        w1_piece(1, w1_raw1a, 256, 80)
-        w1_piece(2, w1_raw1b, 0, 80)
+        def gelu(index):
+            c0, width = PIECES[index]
+            cols = slice(c0, c0 + width)
+            nc.scalar.activation(h[:, cols], acc[index][:, 0:width], GELU)
+            if index == 2:
+                nc.scalar.activation(hb[:, cols], acc[index][:, 0:width], GELU)
+            else:
+                vcopy(hb[:, cols], h[:, cols])
+
+        interleave_piece(0, 160, 0, 2)
+        interleave_piece(0, 160, 2, 4)
+        quantize_piece(0)
+        pass_k(1, 0)
+        interleave_piece(1, 80)
+        quantize_piece(1)
+        pass_k(1, 1)
+        interleave_piece(2, 64)
+        quantize_piece(2)
+        pass_k(1, 2)
+        for index in range(3):
+            gelu(index)
 
         g_bf = keep.tile([P, H], BF16, name="g_bf", align_bytes=64)
         g_view = g_bf[:].rearrange("q (u p e) -> q p u e", u=2, e=2)
-        for half in range(2):
-            nc.vector.tensor_copy(
-                out=g_view[:, 64 * half : 64 * (half + 1)],
-                in_=h[:].indirect(offsets[:, 16 * half : 16 * (half + 1)]),
-            )
+        nc.vector.tensor_copy(out=g_view[:, 0 : 4 * 18], in_=h[:].indirect(offsets[:, 0:18]))
+        nc.scalar.activation(g_view[:, 4 * 18 : P], hb[:].indirect(offsets[:, 18:32]), COPY)
 
-        w2_bf = keep.tile([P, N * PACK], BF16, name="w2_bf", align_bytes=64)
+        w2_bf = keep.tile([P, N * PACK], BF16, name="w2_bf", tag="h", align_bytes=64)
         w2_codes = keep.tile([P, N], U32, name="w2_codes", align_bytes=64)
         w2_scales = keep.tile([P, N], U8, name="w2_scales", align_bytes=64)
-        interleave(scopy, w2_bf, w2_raw, 0, N)
+        interleave(vcopy, w2_bf[:], w2_raw, 0, 192)
+        interleave(scopy, w2_bf[:], w2_raw, 192, N)
         quantize(w2_codes[:], w2_scales[:], w2_bf[:])
 
         words = g_bf[:].bitcast(F32)

@@ -34,10 +34,10 @@ def tile_picked_shuffle_mlp_gelu_perm_l_kernel(tc, xT, w1, w2, offs, out):
     def gcopy(dst, src):
         nc.gpsimd.tensor_scalar(out=dst, in0=src, scalar1=1.0, scalar2=0.0, op0=MULT, op1=ADD)
 
-    def interleave(copy, dst, raw, c0, c1, j0=0, j1=PACK):
+    def interleave(copy, dst, raw, c0, c1, j0=0, base=0):
         copy(
-            dst.rearrange("p (c i j) -> p c j i", i=4, j=PACK)[:, c0 // 4 : c1 // 4, j0:j1],
-            raw[:, j0:j1, c0:c1].rearrange("p j (c i) -> p c j i", i=4),
+            dst.rearrange("p (c i j) -> p c j i", i=4, j=PACK)[:, c0 // 4 : c1 // 4, j0 : j0 + raw.shape[1]],
+            raw[:, :, c0 - base : c1 - base].rearrange("p j (c i) -> p c j i", i=4),
         )
 
     def quantize(codes, scales, grouped):
@@ -50,22 +50,19 @@ def tile_picked_shuffle_mlp_gelu_perm_l_kernel(tc, xT, w1, w2, offs, out):
         offsets = keep.tile([P, H // 16], U16, name="offsets")
         x_raw = keep.tile([P, 2, PACK, T], F32, name="x_raw")
         w1_raw0 = keep.tile([P, PACK, H], F32, name="w1_raw0")
-        w1_raw1 = []
-        for c0, width in PIECES:
-            raw = keep.tile([P, PACK, width], F32, name="w1_raw1_%d" % c0, tag="h" if c0 == 384 else "raw%d" % c0, align_bytes=64)
-            w1_raw1.append(raw)
+        w1_raw1a = keep.tile([P, 2, H], F32, name="w1_raw1a")
+        w1_raw1b = keep.tile([P, 2, 256], F32, name="w1_raw1b")
+        w1_raw1c = keep.tile([P, 2, 256], F32, name="w1_raw1c", tag="h", align_bytes=64)
         w2_raw = keep.tile([P, PACK, N], F32, name="w2_raw")
 
         w1_lo = w1[0:KP, :].rearrange("(p j) c -> p j c", j=PACK)
         nc.sync.dma_start(out=x_raw[:, 0], in_=xT[0:KP, :].rearrange("(p j) t -> p j t", j=PACK))
-        nc.sync.dma_start(out=w1_raw0[:, 0:2], in_=w1_lo[:, 0:2])
-        nc.sync.dma_start(out=w1_raw0[:, 2:4], in_=w1_lo[:, 2:4])
+        nc.sync.dma_start(out=w1_raw0[:], in_=w1_lo)
         nc.sync.dma_start(out=x_raw[:, 1], in_=xT[KP:K, :].rearrange("(p j) t -> p j t", j=PACK))
         w1_hi = w1[KP:K, :].rearrange("(p j) c -> p j c", j=PACK)
-        nc.sync.dma_start(out=w1_raw1[0][:, 0:2], in_=w1_hi[:, 0:2, 0:256])
-        nc.sync.dma_start(out=w1_raw1[0][:, 2:4], in_=w1_hi[:, 2:4, 0:256])
-        nc.sync.dma_start(out=w1_raw1[1][:], in_=w1_hi[:, :, 256:384])
-        nc.sync.dma_start(out=w1_raw1[2][:], in_=w1_hi[:, :, 384:512])
+        nc.sync.dma_start(out=w1_raw1a[:], in_=w1_hi[:, 0:2])
+        nc.sync.dma_start(out=w1_raw1b[:], in_=w1_hi[:, 2:4, 0:256])
+        nc.sync.dma_start(out=w1_raw1c[:], in_=w1_hi[:, 2:4, 256:512])
         nc.sync.dma_start(offsets[:], offs)
         nc.sync.dma_start(out=w2_raw[:], in_=w2.rearrange("(p j) m -> p j m", j=PACK))
 
@@ -88,11 +85,11 @@ def tile_picked_shuffle_mlp_gelu_perm_l_kernel(tc, xT, w1, w2, offs, out):
             cols = slice(g * T, (g + 1) * T)
             quantize(x_codes[:, cols], x_scales[:, cols], x_bf[:, PACK * g * T : PACK * (g + 1) * T])
 
-        interleave(scopy, x_bf[:, 0 : T * PACK], x_raw[:, 0], 0, T)
+        interleave(vcopy, x_bf[:, 0 : T * PACK], x_raw[:, 0], 0, 64)
+        interleave(scopy, x_bf[:, 0 : T * PACK], x_raw[:, 0], 64, T)
         quantize_x(0)
-        for j0 in (0, 2):
-            interleave(vcopy, w1_bf[:, 0], w1_raw0, 0, 320, j0, j0 + 2)
-            interleave(scopy, w1_bf[:, 0], w1_raw0, 320, H, j0, j0 + 2)
+        interleave(vcopy, w1_bf[:, 0], w1_raw0, 0, 352)
+        interleave(scopy, w1_bf[:, 0], w1_raw0, 352, H)
         quantize(w1_codes[:, 0, :], w1_scales[:, 0, :], w1_bf[:, 0, :])
         interleave(vcopy, x_bf[:, T * PACK :], x_raw[:, 1], 0, 64)
         interleave(scopy, x_bf[:, T * PACK :], x_raw[:, 1], 64, T)
@@ -126,12 +123,6 @@ def tile_picked_shuffle_mlp_gelu_perm_l_kernel(tc, xT, w1, w2, offs, out):
         h = keep.tile([P, H], F32, name="h", tag="h", align_bytes=64)
         hb = keep.tile([P, H], BF16, name="hb", align_bytes=64)
 
-        def interleave_piece(index, vector_columns, j0=0, j1=PACK):
-            c0, width = PIECES[index]
-            dst = w1_bf[:, 1, PACK * c0 : PACK * (c0 + width)]
-            interleave(vcopy, dst, w1_raw1[index], 0, vector_columns, j0, j1)
-            interleave(scopy, dst, w1_raw1[index], vector_columns, width, j0, j1)
-
         def gelu(index):
             c0, width = PIECES[index]
             cols = slice(c0, c0 + width)
@@ -141,16 +132,18 @@ def tile_picked_shuffle_mlp_gelu_perm_l_kernel(tc, xT, w1, w2, offs, out):
             else:
                 vcopy(hb[:, cols], h[:, cols])
 
-        interleave_piece(0, 160, 0, 2)
-        interleave_piece(0, 160, 2, 4)
-        quantize_piece(0)
-        pass_k(1, 0)
-        interleave_piece(1, 80)
-        quantize_piece(1)
-        pass_k(1, 1)
-        interleave_piece(2, 64)
-        quantize_piece(2)
-        pass_k(1, 2)
+        w1_hi_bf = w1_bf[:, 1]
+        interleave(vcopy, w1_hi_bf, w1_raw1a, 0, 352)
+        interleave(scopy, w1_hi_bf, w1_raw1a, 352, H)
+        for raw, base, cuts, index in (
+            (w1_raw1b, 0, (0, 160, 256), 0),
+            (w1_raw1c, 256, (256, 320, 384), 1),
+            (w1_raw1c, 256, (384, 448, 512), 2),
+        ):
+            interleave(vcopy, w1_hi_bf, raw, cuts[0], cuts[1], 2, base)
+            interleave(scopy, w1_hi_bf, raw, cuts[1], cuts[2], 2, base)
+            quantize_piece(index)
+            pass_k(1, index)
         for index in range(3):
             gelu(index)
 

@@ -14,7 +14,6 @@ U8 = mybir.dt.uint8
 FP8X4 = mybir.dt.float8_e4m3fn_x4
 GELU = mybir.ActivationFunctionType.Gelu_apprx_tanh
 COPY = mybir.ActivationFunctionType.Copy
-MULT, ADD = mybir.AluOpType.mult, mybir.AluOpType.add
 
 P = 128
 PACK = 4
@@ -31,13 +30,10 @@ def tile_picked_shuffle_mlp_gelu_perm_l_kernel(tc, xT, w1, w2, offs, out):
     def scopy(dst, src):
         nc.scalar.copy(dst, src)
 
-    def gcopy(dst, src):
-        nc.gpsimd.tensor_scalar(out=dst, in0=src, scalar1=1.0, scalar2=0.0, op0=MULT, op1=ADD)
-
-    def interleave(copy, dst, raw, c0, c1, j0=0, base=0):
+    def interleave(copy, dst, raw, c0, c1):
         copy(
-            dst.rearrange("p (c i j) -> p c j i", i=4, j=PACK)[:, c0 // 4 : c1 // 4, j0 : j0 + raw.shape[1]],
-            raw[:, :, c0 - base : c1 - base].rearrange("p j (c i) -> p c j i", i=4),
+            dst[:, PACK * c0 : PACK * c1].rearrange("p (c i j) -> p c j i", i=4, j=PACK),
+            raw[:, :, c0:c1].rearrange("p j (c i) -> p c j i", i=4),
         )
 
     def quantize(codes, scales, grouped):
@@ -49,20 +45,24 @@ def tile_picked_shuffle_mlp_gelu_perm_l_kernel(tc, xT, w1, w2, offs, out):
 
         offsets = keep.tile([P, H // 16], U16, name="offsets")
         x_raw = keep.tile([P, 2, PACK, T], F32, name="x_raw")
-        w1_raw0 = keep.tile([P, PACK, H], F32, name="w1_raw0")
-        w1_raw1a = keep.tile([P, 2, H], F32, name="w1_raw1a")
-        w1_raw1b = keep.tile([P, 2, 256], F32, name="w1_raw1b")
-        w1_raw1c = keep.tile([P, 2, 256], F32, name="w1_raw1c", tag="h", align_bytes=64)
+        w1_raw0 = []
+        for c0 in (0, 256):
+            raw = keep.tile([P, PACK, 256], F32, name="w1_raw0_%d" % c0)
+            w1_raw0.append(raw)
+        w1_raw1 = []
+        for c0, width in PIECES:
+            raw = keep.tile([P, PACK, width], F32, name="w1_raw1_%d" % c0, tag="h" if c0 == 384 else "w1_raw1_%d" % c0, align_bytes=64)
+            w1_raw1.append(raw)
         w2_raw = keep.tile([P, PACK, N], F32, name="w2_raw")
 
         w1_lo = w1[0:KP, :].rearrange("(p j) c -> p j c", j=PACK)
         nc.sync.dma_start(out=x_raw[:, 0], in_=xT[0:KP, :].rearrange("(p j) t -> p j t", j=PACK))
-        nc.sync.dma_start(out=w1_raw0[:], in_=w1_lo)
+        nc.sync.dma_start(out=w1_raw0[0][:], in_=w1_lo[:, :, 0:256])
+        nc.sync.dma_start(out=w1_raw0[1][:], in_=w1_lo[:, :, 256:512])
         nc.sync.dma_start(out=x_raw[:, 1], in_=xT[KP:K, :].rearrange("(p j) t -> p j t", j=PACK))
         w1_hi = w1[KP:K, :].rearrange("(p j) c -> p j c", j=PACK)
-        nc.sync.dma_start(out=w1_raw1a[:], in_=w1_hi[:, 0:2])
-        nc.sync.dma_start(out=w1_raw1b[:], in_=w1_hi[:, 2:4, 0:256])
-        nc.sync.dma_start(out=w1_raw1c[:], in_=w1_hi[:, 2:4, 256:512])
+        for raw, (c0, width) in zip(w1_raw1, PIECES):
+            nc.sync.dma_start(out=raw[:], in_=w1_hi[:, :, c0 : c0 + width])
         nc.sync.dma_start(offsets[:], offs)
         nc.sync.dma_start(out=w2_raw[:], in_=w2.rearrange("(p j) m -> p j m", j=PACK))
 
@@ -85,16 +85,6 @@ def tile_picked_shuffle_mlp_gelu_perm_l_kernel(tc, xT, w1, w2, offs, out):
             cols = slice(g * T, (g + 1) * T)
             quantize(x_codes[:, cols], x_scales[:, cols], x_bf[:, PACK * g * T : PACK * (g + 1) * T])
 
-        interleave(vcopy, x_bf[:, 0 : T * PACK], x_raw[:, 0], 0, 64)
-        interleave(scopy, x_bf[:, 0 : T * PACK], x_raw[:, 0], 64, T)
-        quantize_x(0)
-        interleave(vcopy, w1_bf[:, 0], w1_raw0, 0, 352)
-        interleave(scopy, w1_bf[:, 0], w1_raw0, 352, H)
-        quantize(w1_codes[:, 0, :], w1_scales[:, 0, :], w1_bf[:, 0, :])
-        interleave(vcopy, x_bf[:, T * PACK :], x_raw[:, 1], 0, 64)
-        interleave(scopy, x_bf[:, T * PACK :], x_raw[:, 1], 64, T)
-        quantize_x(1)
-
         acc = []
         for c0, width in PIECES:
             bank = psum.tile([P, 512], F32, name="acc%d" % c0)
@@ -112,17 +102,6 @@ def tile_picked_shuffle_mlp_gelu_perm_l_kernel(tc, xT, w1, w2, offs, out):
                 stop=(g == 1),
             )
 
-        def quantize_piece(index):
-            c0, width = PIECES[index]
-            cols = slice(c0, c0 + width)
-            quantize(w1_codes[:, 1, cols], w1_scales[:, 1, cols], w1_bf[:, 1, PACK * c0 : PACK * (c0 + width)])
-
-        for index in range(len(PIECES)):
-            pass_k(0, index)
-
-        h = keep.tile([P, H], F32, name="h", tag="h", align_bytes=64)
-        hb = keep.tile([P, H], BF16, name="hb", align_bytes=64)
-
         def gelu(index):
             c0, width = PIECES[index]
             cols = slice(c0, c0 + width)
@@ -132,18 +111,38 @@ def tile_picked_shuffle_mlp_gelu_perm_l_kernel(tc, xT, w1, w2, offs, out):
             else:
                 vcopy(hb[:, cols], h[:, cols])
 
-        w1_hi_bf = w1_bf[:, 1]
-        interleave(vcopy, w1_hi_bf, w1_raw1a, 0, 352)
-        interleave(scopy, w1_hi_bf, w1_raw1a, 352, H)
-        for raw, base, cuts, index in (
-            (w1_raw1b, 0, (0, 160, 256), 0),
-            (w1_raw1c, 256, (256, 320, 384), 1),
-            (w1_raw1c, 256, (384, 448, 512), 2),
-        ):
-            interleave(vcopy, w1_hi_bf, raw, cuts[0], cuts[1], 2, base)
-            interleave(scopy, w1_hi_bf, raw, cuts[1], cuts[2], 2, base)
-            quantize_piece(index)
+        def interleave_x(g, split):
+            dst = x_bf[:, PACK * g * T : PACK * (g + 1) * T]
+            interleave(vcopy, dst, x_raw[:, g], 0, split)
+            interleave(scopy, dst, x_raw[:, g], split, T)
+
+        def interleave_w1(g, c0, width, raw, split):
+            dst = w1_bf[:, g, PACK * c0 : PACK * (c0 + width)]
+            interleave(vcopy, dst, raw, 0, split)
+            interleave(scopy, dst, raw, split, width)
+
+        def quantize_w1(g, c0, width):
+            cols = slice(c0, c0 + width)
+            quantize(w1_codes[:, g, cols], w1_scales[:, g, cols], w1_bf[:, g, PACK * c0 : PACK * (c0 + width)])
+
+        interleave_x(0, 80)
+        quantize_x(0)
+        interleave_w1(0, 0, 256, w1_raw0[0], 176)
+        quantize_w1(0, 0, 256)
+        interleave_w1(0, 256, 256, w1_raw0[1], 176)
+        pass_k(0, 0)
+        quantize_w1(0, 256, 256)
+        interleave_x(1, 80)
+        quantize_x(1)
+        pass_k(0, 1)
+        pass_k(0, 2)
+        for index, split in enumerate((176, 80, 76)):
+            c0, width = PIECES[index]
+            interleave_w1(1, c0, width, w1_raw1[index], split)
+            quantize_w1(1, c0, width)
             pass_k(1, index)
+        h = keep.tile([P, H], F32, name="h", tag="h", align_bytes=64)
+        hb = keep.tile([P, H], BF16, name="hb", align_bytes=64)
         for index in range(3):
             gelu(index)
 

from contextlib import ExitStack

import concourse.mybir as mybir
from concourse.masks import make_identity

K, T, H, N = 1024, 128, 512, 256
FLOPS = 2 * K * T * H + 2 * H * T * N

F32 = mybir.dt.float32
BF16 = mybir.dt.bfloat16
U32 = mybir.dt.uint32
U16 = mybir.dt.uint16
U8 = mybir.dt.uint8
FP8X4 = mybir.dt.float8_e4m3fn_x4
GELU = mybir.ActivationFunctionType.Gelu_apprx_tanh
COPY = mybir.ActivationFunctionType.Copy

P = 128
PACK = 4
KP = 512

PIECES = ((0, 256), (256, 128), (384, 128))

def tile_picked_shuffle_mlp_gelu_perm_l_kernel(tc, xT, w1, w2, offs, out):
    nc = tc.nc

    def vcopy(dst, src):
        nc.vector.tensor_copy(out=dst, in_=src)

    def scopy(dst, src):
        nc.scalar.copy(dst, src)

    def interleave(copy, dst, raw, c0, c1):
        copy(
            dst[:, PACK * c0 : PACK * c1].rearrange("p (c i j) -> p c j i", i=4, j=PACK),
            raw[:, :, c0:c1].rearrange("p j (c i) -> p c j i", i=4),
        )

    def quantize(codes, scales, grouped):
        nc.vector.quantize_mx(out=codes.bitcast(FP8X4), scales=scales, in_=grouped)

    with ExitStack() as ctx:
        keep = ctx.enter_context(tc.tile_pool(name="keep", bufs=1))
        psum = ctx.enter_context(tc.psum_pool(name="psum", bufs=1))

        offsets = keep.tile([P, H // 16], U16, name="offsets")
        x_raw = keep.tile([P, 2, PACK, T], F32, name="x_raw")
        w1_raw0 = []
        for c0 in (0, 256):
            raw = keep.tile([P, PACK, 256], F32, name="w1_raw0_%d" % c0)
            w1_raw0.append(raw)
        w1_raw1 = []
        for c0, width in PIECES:
            raw = keep.tile([P, PACK, width], F32, name="w1_raw1_%d" % c0, tag="h" if c0 == 384 else "w1_raw1_%d" % c0, align_bytes=64)
            w1_raw1.append(raw)
        w2_raw = keep.tile([P, PACK, N], F32, name="w2_raw")

        w1_lo = w1[0:KP, :].rearrange("(p j) c -> p j c", j=PACK)
        nc.sync.dma_start(out=x_raw[:, 0], in_=xT[0:KP, :].rearrange("(p j) t -> p j t", j=PACK))
        nc.sync.dma_start(out=w1_raw0[0][:], in_=w1_lo[:, :, 0:256])
        nc.sync.dma_start(out=w1_raw0[1][:], in_=w1_lo[:, :, 256:512])
        nc.sync.dma_start(out=x_raw[:, 1], in_=xT[KP:K, :].rearrange("(p j) t -> p j t", j=PACK))
        w1_hi = w1[KP:K, :].rearrange("(p j) c -> p j c", j=PACK)
        for raw, (c0, width) in zip(w1_raw1, PIECES):
            nc.sync.dma_start(out=raw[:], in_=w1_hi[:, :, c0 : c0 + width])
        nc.sync.dma_start(offsets[:], offs)
        nc.sync.dma_start(out=w2_raw[:], in_=w2.rearrange("(p j) m -> p j m", j=PACK))

        warm = keep.tile([P, 1], F32, name="warm")
        warm_out = keep.tile([P, 1], F32, name="warm_out")
        nc.vector.memset(warm[:], 0.0)
        nc.scalar.activation(warm_out[:], warm[:], GELU)

        ident = keep.tile([P, P], F32, name="ident")
        make_identity(nc, ident[:])

        x_bf = keep.tile([P, 2 * T * PACK], BF16, name="x_bf", align_bytes=64)
        x_codes = keep.tile([P, 2 * T], U32, name="x_codes", align_bytes=64)
        x_scales = keep.tile([P, 2 * T], U8, name="x_scales", align_bytes=64)
        w1_bf = keep.tile([P, 2, H * PACK], BF16, name="w1_bf", align_bytes=64)
        w1_codes = keep.tile([P, 2, H], U32, name="w1_codes", align_bytes=64)
        w1_scales = keep.tile([P, 2, H], U8, name="w1_scales", align_bytes=64)

        def quantize_x(g):
            cols = slice(g * T, (g + 1) * T)
            quantize(x_codes[:, cols], x_scales[:, cols], x_bf[:, PACK * g * T : PACK * (g + 1) * T])

        acc = []
        for c0, width in PIECES:
            bank = psum.tile([P, 512], F32, name="acc%d" % c0)
            acc.append(bank)

        def pass_k(g, index):
            c0, width = PIECES[index]
            nc.tensor.matmul_mx(
                out=acc[index][:, 0:width],
                lhsT=x_codes[:, g * T : (g + 1) * T].bitcast(FP8X4),
                lhsT_scale=x_scales[:, g * T : (g + 1) * T],
                rhs=w1_codes[:, g, c0 : c0 + width].bitcast(FP8X4),
                rhs_scale=w1_scales[:, g, c0 : c0 + width],
                start=(g == 0),
                stop=(g == 1),
            )

        def gelu(index):
            c0, width = PIECES[index]
            cols = slice(c0, c0 + width)
            nc.scalar.activation(h[:, cols], acc[index][:, 0:width], GELU)
            if index == 2:
                nc.scalar.activation(hb[:, cols], acc[index][:, 0:width], GELU)
            else:
                vcopy(hb[:, cols], h[:, cols])

        def interleave_x(g, split):
            dst = x_bf[:, PACK * g * T : PACK * (g + 1) * T]
            interleave(vcopy, dst, x_raw[:, g], 0, split)
            interleave(scopy, dst, x_raw[:, g], split, T)

        def interleave_w1(g, c0, width, raw, split):
            dst = w1_bf[:, g, PACK * c0 : PACK * (c0 + width)]
            interleave(vcopy, dst, raw, 0, split)
            interleave(scopy, dst, raw, split, width)

        def quantize_w1(g, c0, width):
            cols = slice(c0, c0 + width)
            quantize(w1_codes[:, g, cols], w1_scales[:, g, cols], w1_bf[:, g, PACK * c0 : PACK * (c0 + width)])

        interleave_x(0, 80)
        quantize_x(0)
        interleave_w1(0, 0, 256, w1_raw0[0], 176)
        quantize_w1(0, 0, 256)
        interleave_w1(0, 256, 256, w1_raw0[1], 176)
        pass_k(0, 0)
        quantize_w1(0, 256, 256)
        interleave_x(1, 80)
        quantize_x(1)
        pass_k(0, 1)
        pass_k(0, 2)
        for index, split in enumerate((176, 80, 76)):
            c0, width = PIECES[index]
            interleave_w1(1, c0, width, w1_raw1[index], split)
            quantize_w1(1, c0, width)
            pass_k(1, index)
        h = keep.tile([P, H], F32, name="h", tag="h", align_bytes=64)
        hb = keep.tile([P, H], BF16, name="hb", align_bytes=64)
        for index in range(3):
            gelu(index)

        g_bf = keep.tile([P, H], BF16, name="g_bf", align_bytes=64)
        g_view = g_bf[:].rearrange("q (u p e) -> q p u e", u=2, e=2)
        nc.vector.tensor_copy(out=g_view[:, 0 : 4 * 18], in_=h[:].indirect(offsets[:, 0:18]))
        nc.scalar.activation(g_view[:, 4 * 18 : P], hb[:].indirect(offsets[:, 18:32]), COPY)

        w2_bf = keep.tile([P, N * PACK], BF16, name="w2_bf", tag="h", align_bytes=64)
        w2_codes = keep.tile([P, N], U32, name="w2_codes", align_bytes=64)
        w2_scales = keep.tile([P, N], U8, name="w2_scales", align_bytes=64)
        interleave(vcopy, w2_bf[:], w2_raw, 0, 192)
        interleave(scopy, w2_bf[:], w2_raw, 192, N)
        quantize(w2_codes[:], w2_scales[:], w2_bf[:])

        words = g_bf[:].bitcast(F32)
        turned = psum.tile([P, 2, P], F32, name="turned")
        for u in range(2):
            nc.tensor.transpose(turned[:, u, :], words[:, 128 * u : 128 * (u + 1)], ident[:])
        h_bf = keep.tile([P, T * PACK], BF16, name="h_bf", align_bytes=64)
        nc.scalar.copy(h_bf[:].bitcast(F32).rearrange("p (t u) -> p t u", u=2), turned[:].rearrange("p u t -> p t u"))
        h_codes = keep.tile([P, T], U32, name="h_codes", align_bytes=64)
        h_scales = keep.tile([P, T], U8, name="h_scales", align_bytes=64)
        quantize(h_codes[:], h_scales[:], h_bf[:])

        for m, copy, dma in ((0, vcopy, nc.sync), (1, scopy, nc.scalar)):
            bank = psum.tile([P, 512], F32, name="out_bank%d" % m)
            cols = slice(P * m, P * (m + 1))
            nc.tensor.matmul_mx(
                out=bank[:, 0:T],
                lhsT=w2_codes[:, cols].bitcast(FP8X4),
                lhsT_scale=w2_scales[:, cols],
                rhs=h_codes[:].bitcast(FP8X4),
                rhs_scale=h_scales[:],
                start=True,
                stop=True,
            )
            y = keep.tile([P, T], F32, name="y%d" % m)
            copy(y[:], bank[:, 0:T])
            dma.dma_start(out=out[cols, :], in_=y[:])
